import numpy as np
import ml_dtypes


def mxq(x, axis, fmt="e4m3"):
    dtype, down = {"e4m3": (ml_dtypes.float8_e4m3fn, 7), "e5m2": (ml_dtypes.float8_e5m2, 14)}[fmt]
    v = np.moveaxis(np.asarray(x, np.float32).astype(ml_dtypes.bfloat16).astype(np.float64), axis, -1)
    blocks = v.reshape(v.shape[:-1] + (-1, 32))
    amax = np.abs(blocks).max(-1, keepdims=True)
    byte = np.maximum(np.where(amax > 0, np.frexp(amax)[1] - 1 + 127, 0) - down, 1)
    scale = np.exp2(byte - 127.0)
    codes = (blocks / scale).astype(np.float32).astype(dtype).astype(np.float64)
    return np.moveaxis((codes * scale).reshape(v.shape), -1, axis)


WIDE = False


def mx_kscale(k):
    if not WIDE:
        return np.ones(k)
    levels = np.array([10, -10, 5, -5, 0])
    if k % 512:
        return np.exp2(np.random.permutation(np.resize(levels, k // 32))).repeat(32)
    a = np.empty((k // 512, 16))
    for p in range(k // 512):
        a[p, :8] = np.random.permutation(np.resize(levels, 8))
        for g in range(8):
            far = levels[np.abs(levels - a[p, g]) >= 10]
            a[p, g + 8] = far[np.random.randint(len(far))]
    return np.exp2(a.ravel()).repeat(32)


def f64(x):
    return np.asarray(x).astype(np.float64)


def striped(idx):
    return np.tile(np.asarray(idx).reshape(-1, 16).T, (8, 1)).astype(np.uint16)


def unstriped(offs):
    return offs[:16].T.reshape(-1).astype(np.int64)


B, N, T, D, DV, NQ = 1, 512, 1024, 512, 256, 128
CAP = 2.0
DRAFT = 128


def setup_inputs():
    n = np.random.standard_normal
    idx = np.random.permutation(T)[:B * N]
    s = mx_kscale(D)[:, None]
    u = np.ones(T)
    u[idx] = mx_kscale(B * N)
    r = np.random.uniform(0.5, 2.0, T)
    k = n((D, T)) / s
    v = n((DV, T)) / (u * r)
    when = np.zeros(T)
    when[idx] = np.concatenate([np.concatenate([np.arange(N - DRAFT), N - DRAFT + np.random.randint(0, 16, DRAFT)]) for b in range(B)])
    return {
        "qT": (n((B, D, NQ)) * s * (0.80 / np.sqrt(D))).astype(np.float32),
        "kT": k.astype(np.float32),
        "vT": v.astype(np.float32),
        "vs": np.tile(u * r, (128, 1)).astype(np.float32),
        "pos": np.tile(when, (128, 1)).astype(np.float32),
        "qpos": np.random.randint(N - DRAFT, N - DRAFT + 16, (B, NQ, 1)).astype(np.float32),
        "offs": striped(idx),
    }


def reference(qT, kT, vT, vs, pos, qpos, offs):
    idx = unstriped(offs)
    k = f64(kT)
    v = f64(vT)
    pick = lambda x: x[:, idx].reshape(x.shape[0], B, N).transpose(1, 0, 2)
    q = f64(qT)
    score = mxq(q, 1, "e4m3").transpose(0, 2, 1) @ mxq(pick(k), 1, "e4m3")
    score = CAP * np.tanh(score / CAP)
    score = np.where(pick(f64(pos))[:, :1, :] <= f64(qpos), score, -30000.0)
    m = score.max(-1, keepdims=True)
    p = np.exp(score - m)
    total = p.sum(-1, keepdims=True)
    w = p * pick(f64(vs))[:, :1, :]
    y = mxq(w, 2, "e4m3") @ mxq(pick(v).transpose(0, 2, 1), 1, "e4m3")
    y = y / total
    return y

@@ -1,0 +1,178 @@
+from contextlib import ExitStack
+
+import concourse.mybir as mybir
+from concourse.masks import make_identity
+
+D, T, N, DV, NQ = 512, 1024, 512, 256, 128
+CAP = 2.0
+MASKED = -30000.0
+FLOPS = 2 * D * NQ * N + 2 * N * NQ * DV
+
+P = 128
+PACK = 4
+HALF = N // 2
+CHUNK = T // 2
+
+F32 = mybir.dt.float32
+BF16 = mybir.dt.bfloat16
+U32 = mybir.dt.uint32
+U16 = mybir.dt.uint16
+U8 = mybir.dt.uint8
+FP8X4 = mybir.dt.float8_e4m3fn_x4
+ALU = mybir.AluOpType
+ACT = mybir.ActivationFunctionType
+AX = mybir.AxisListType
+
+
+def tile_attend_x_draft_cap_topk_kernel(tc, qT, kT, vT, vs, pos, qpos, offs, out):
+    nc = tc.nc
+    with ExitStack() as ctx:
+        keep = ctx.enter_context(tc.tile_pool(name="keep", bufs=1))
+        psum = ctx.enter_context(tc.psum_pool(name="psum", bufs=1))
+
+        offsets = keep.tile([P, N // 16], U16, name="offsets")
+        nc.sync.dma_start(offsets[:], offs)
+        qpos_col = keep.tile([P, 1], F32, name="qpos_col")
+        nc.scalar.dma_start(out=qpos_col[:], in_=qpos.rearrange("b q o -> (b q) o"))
+        pos_pool = keep.tile([P, T], F32, name="pos_pool")
+        vs_pool = keep.tile([P, T], F32, name="vs_pool")
+        q_raw = keep.tile([P, PACK, NQ], F32, name="q_raw")
+        k_rows = kT.rearrange("(p j) t -> p j t", j=PACK)
+        v_rows = vT.rearrange("(p h) t -> p h t", h=2)
+        k_raw = {(u, c): keep.tile([P, 2, CHUNK], F32, name=f"k_raw{u}{c}") for u in range(2) for c in range(2)}
+        v_raw = [keep.tile([P, 2, CHUNK], F32, name=f"v_raw{c}") for c in range(2)]
+
+        def load_k(u, c):
+            nc.sync.dma_start(out=k_raw[u, c][:], in_=k_rows[:, 2 * u : 2 * u + 2, c * CHUNK : (c + 1) * CHUNK])
+
+        def load_v(c):
+            nc.sync.dma_start(out=v_raw[c][:], in_=v_rows[:, :, c * CHUNK : (c + 1) * CHUNK])
+
+        nc.sync.dma_start(out=pos_pool[:], in_=pos)
+        load_k(0, 0)
+        load_k(0, 1)
+        load_k(1, 0)
+        load_k(1, 1)
+        nc.sync.dma_start(out=q_raw[:], in_=qT.rearrange("b (p j) q -> p (b j) q", j=PACK))
+        load_v(0)
+        nc.sync.dma_start(out=vs_pool[:], in_=vs)
+        load_v(1)
+
+        warm = keep.tile([P, 1], F32, name="warm")
+        nc.gpsimd.memset(warm[:], 0.0)
+        warm_out = keep.tile([P, 1], F32, name="warm_out")
+        nc.scalar.activation(out=warm_out[:], in_=warm[:], func=ACT.Exp)
+        ident = keep.tile([P, P], F32, name="ident")
+        make_identity(nc, ident[:])
+
+        pos_g = keep.tile([P, N], F32, name="pos_g")
+        seen = keep.tile([P, N], F32, name="seen")
+        bound = keep.tile([P, N], F32, name="bound")
+        k_pairs = [keep.tile([P, 2 * T], BF16, name=f"k_pairs{u}", align_bytes=64) for u in range(2)]
+        k_got = keep.tile([P, PACK * N], BF16, name="k_got", align_bytes=64)
+        k_got_words = k_got[:].bitcast(U32).rearrange("p (s u) -> p s u", u=2)
+        v_pairs = keep.tile([P, 2 * T], BF16, name="v_pairs", align_bytes=64)
+        v_got = keep.tile([P, 2 * N], BF16, name="v_got", align_bytes=64)
+        v_words = v_got[:].bitcast(F32)
+        v_turned = psum.tile([P, PACK, P], F32, name="v_turned")
+        v_bf = keep.tile([P, DV * PACK], BF16, name="v_bf", align_bytes=64)
+        v_codes = keep.tile([P, DV], U32, name="v_codes", align_bytes=64)
+        v_scales = keep.tile([P, DV], U8, name="v_scales", align_bytes=64)
+        q_bf = keep.tile([P, NQ * PACK], BF16, name="q_bf", align_bytes=64)
+        q_codes = keep.tile([P, NQ], U32, name="q_codes", align_bytes=64)
+        q_scales = keep.tile([P, NQ], U8, name="q_scales", align_bytes=64)
+        k_codes = [keep.tile([P, HALF], U32, name=f"k_codes{h}", align_bytes=64) for h in range(2)]
+        k_scales = [keep.tile([P, HALF], U8, name=f"k_scales{h}", align_bytes=64) for h in range(2)]
+        score = [psum.tile([NQ, HALF], F32, name=f"score{h}") for h in range(2)]
+        vs_g = keep.tile([P, N], F32, name="vs_g")
+        capped = keep.tile([NQ, N], F32, name="capped")
+        visible = keep.tile([NQ, N], F32, name="visible")
+        neg_max = keep.tile([NQ, 1], F32, name="neg_max")
+        prob = keep.tile([NQ, N], F32, name="prob")
+        sums = [keep.tile([NQ, 1], F32, name=f"row_sum{h}") for h in range(2)]
+        weight = keep.tile([NQ, N], BF16, name="weight", align_bytes=64)
+        w_turned = psum.tile([P, 2, NQ], F32, name="w_turned")
+        w_words = weight[:].bitcast(F32)
+        w_bf = keep.tile([P, NQ * PACK], BF16, name="w_bf", align_bytes=64)
+        w_codes = keep.tile([P, NQ], U32, name="w_codes", align_bytes=64)
+        w_scales = keep.tile([P, NQ], U8, name="w_scales", align_bytes=64)
+        row_sum = keep.tile([NQ, 1], F32, name="row_sum")
+        inverse = keep.tile([NQ, 1], F32, name="inverse")
+        y = psum.tile([NQ, DV], F32, name="y")
+        result = keep.tile([NQ, DV], F32, name="result")
+
+        def cast(engine, pairs, raw, first, a, b):
+            dst = pairs[:, 2 * (first + a) : 2 * (first + b)].rearrange("p (t h) -> p t h", h=2)
+            src = raw[:, :, a:b].rearrange("p h t -> p t h")
+            if engine == "scalar":
+                nc.scalar.copy(out=dst, in_=src)
+            else:
+                nc.vector.tensor_copy(out=dst, in_=src)
+
+        def half(h):
+            return slice(h * HALF, (h + 1) * HALF)
+
+        def mul_scores(h):
+            nc.tensor.matmul_mx(
+                out=score[h][:], lhsT=q_codes[:].bitcast(FP8X4), lhsT_scale=q_scales[:],
+                rhs=k_codes[h][:].bitcast(FP8X4), rhs_scale=k_scales[h][:], start=True, stop=True,
+            )
+
+        def gather_k1(h):
+            nc.vector.tensor_copy(
+                k_got_words[:, half(h), 1],
+                k_pairs[1][:].bitcast(U32).indirect(offsets[:, h * HALF // 16 : (h + 1) * HALF // 16]),
+            )
+
+        def quant_k(h):
+            nc.vector.quantize_mx(out=k_codes[h][:].bitcast(FP8X4), scales=k_scales[h][:], in_=k_got[:, h * PACK * HALF : (h + 1) * PACK * HALF])
+
+        nc.vector.tensor_copy(pos_g[:], pos_pool[:].indirect(offsets[:]))
+        nc.vector.tensor_scalar(out=seen[:], in0=pos_g[:], scalar1=qpos_col[:, 0:1], scalar2=CAP - MASKED, op0=ALU.is_le, op1=ALU.mult)
+        nc.scalar.activation(out=bound[:], in_=seen[:], func=ACT.Copy, bias=MASKED)
+        cast("vector", k_pairs[0], k_raw[0, 0], 0 * CHUNK, 0, 512)
+        cast("vector", k_pairs[0], k_raw[0, 1], 1 * CHUNK, 0, 512)
+        nc.vector.tensor_copy(k_got_words[:, :, 0], k_pairs[0][:].bitcast(U32).indirect(offsets[:]))
+        cast("scalar", k_pairs[1], k_raw[1, 0], 0 * CHUNK, 0, 512)
+        cast("vector", k_pairs[1], k_raw[1, 1], 1 * CHUNK, 0, 384)
+        cast("scalar", k_pairs[1], k_raw[1, 1], 1 * CHUNK, 384, 512)
+        gather_k1(1)
+        nc.scalar.copy(out=q_bf[:].rearrange("p (q j) -> p q j", j=PACK), in_=q_raw[:].rearrange("p j q -> p q j"))
+        quant_k(1)
+        nc.vector.quantize_mx(out=q_codes[:].bitcast(FP8X4), scales=q_scales[:], in_=q_bf[:])
+        gather_k1(0)
+        quant_k(0)
+        mul_scores(0)
+        mul_scores(1)
+        cast("scalar", v_pairs, v_raw[0], 0 * CHUNK, 0, 512)
+        nc.vector.tensor_copy(vs_g[:], vs_pool[:].indirect(offsets[:]))
+        nc.scalar.activation(out=capped[:, half(0)], in_=score[0][:], func=ACT.Tanh, scale=1.0 / CAP)
+        nc.scalar.activation(out=capped[:, half(1)], in_=score[1][:], func=ACT.Tanh, scale=1.0 / CAP)
+        nc.vector.scalar_tensor_tensor(out=visible[:, half(0)], in0=capped[:, half(0)], scalar=CAP, in1=bound[:, half(0)], op0=ALU.mult, op1=ALU.min)
+        nc.vector.scalar_tensor_tensor(out=visible[:, half(1)], in0=capped[:, half(1)], scalar=CAP, in1=bound[:, half(1)], op0=ALU.mult, op1=ALU.min)
+        nc.vector.tensor_reduce(out=neg_max[:], in_=visible[:], axis=AX.X, op=ALU.max, negate=True)
+        cast("scalar", v_pairs, v_raw[1], 1 * CHUNK, 0, 512)
+        nc.scalar.activation(out=prob[:, half(0)], in_=visible[:, half(0)], func=ACT.Exp, bias=neg_max[:, 0:1], accum_out=sums[0][:])
+        nc.scalar.activation(out=prob[:, half(1)], in_=visible[:, half(1)], func=ACT.Exp, bias=neg_max[:, 0:1], accum_out=sums[1][:])
+        nc.vector.tensor_copy(v_got[:].bitcast(U32).rearrange("p (t s) -> p s t", t=PACK), v_pairs[:].bitcast(U32).indirect(offsets[:]))
+        for t in range(PACK):
+            nc.tensor.transpose(v_turned[:, t, :], v_words[:, t * P : (t + 1) * P], ident[:])
+        nc.vector.tensor_tensor(out=weight[:, half(0)], in0=prob[:, half(0)], in1=vs_g[:, half(0)], op=ALU.mult)
+        nc.vector.tensor_tensor(out=weight[:, half(1)], in0=prob[:, half(1)], in1=vs_g[:, half(1)], op=ALU.mult)
+        for u in range(2):
+            nc.tensor.transpose(w_turned[:, u, :], w_words[:, u::2], ident[:])
+        nc.scalar.copy(
+            out=v_bf[:].rearrange("p (e t) -> p e t", t=PACK),
+            in_=v_turned[:].rearrange("p t w -> p (t w)").bitcast(BF16).rearrange("p (t e) -> p e t", t=PACK),
+        )
+        nc.vector.tensor_copy(out=w_bf[:].bitcast(F32).rearrange("p (q u) -> p q u", u=2), in_=w_turned[:].rearrange("p u q -> p q u"))
+        nc.vector.quantize_mx(out=w_codes[:].bitcast(FP8X4), scales=w_scales[:], in_=w_bf[:])
+        nc.vector.quantize_mx(out=v_codes[:].bitcast(FP8X4), scales=v_scales[:], in_=v_bf[:])
+        nc.vector.tensor_tensor(out=row_sum[:], in0=sums[0][:], in1=sums[1][:], op=ALU.add)
+        nc.vector.reciprocal(out=inverse[:], in_=row_sum[:])
+        nc.tensor.matmul_mx(
+            out=y[:], lhsT=w_codes[:].bitcast(FP8X4), lhsT_scale=w_scales[:],
+            rhs=v_codes[:].bitcast(FP8X4), rhs_scale=v_scales[:], start=True, stop=True,
+        )
+        nc.vector.tensor_scalar(out=result[:], in0=y[:], scalar1=inverse[:, 0:1], scalar2=None, op0=ALU.mult)
+        nc.sync.dma_start(out=out.rearrange("b q e -> (b q) e"), in_=result[:])

@@ -31,12 +31,10 @@ def tile_attend_x_draft_cap_topk_kernel(tc, qT, kT, vT, vs, pos, qpos, offs, out
         psum = ctx.enter_context(tc.psum_pool(name="psum", bufs=1))
 
         offsets = keep.tile([P, N // 16], U16, name="offsets")
-        nc.sync.dma_start(offsets[:], offs)
         qpos_col = keep.tile([P, 1], F32, name="qpos_col")
-        nc.scalar.dma_start(out=qpos_col[:], in_=qpos.rearrange("b q o -> (b q) o"))
         pos_pool = keep.tile([P, T], F32, name="pos_pool")
         vs_pool = keep.tile([P, T], F32, name="vs_pool")
-        q_raw = keep.tile([P, PACK, NQ], F32, name="q_raw")
+        q_raw = keep.tile([P, PACK, NQ], F32, name="q_raw", tag="q_raw")
         k_rows = kT.rearrange("(p j) t -> p j t", j=PACK)
         v_rows = vT.rearrange("(p h) t -> p h t", h=2)
         k_raw = {(u, c): keep.tile([P, 2, CHUNK], F32, name=f"k_raw{u}{c}") for u in range(2) for c in range(2)}
@@ -49,10 +47,12 @@ def tile_attend_x_draft_cap_topk_kernel(tc, qT, kT, vT, vs, pos, qpos, offs, out
             nc.sync.dma_start(out=v_raw[c][:], in_=v_rows[:, :, c * CHUNK : (c + 1) * CHUNK])
 
         nc.sync.dma_start(out=pos_pool[:], in_=pos)
+        nc.sync.dma_start(offsets[:], offs)
         load_k(0, 0)
         load_k(0, 1)
         load_k(1, 0)
         load_k(1, 1)
+        nc.sync.dma_start(out=qpos_col[:], in_=qpos.rearrange("b q o -> (b q) o"))
         nc.sync.dma_start(out=q_raw[:], in_=qT.rearrange("b (p j) q -> p (b j) q", j=PACK))
         load_v(0)
         nc.sync.dma_start(out=vs_pool[:], in_=vs)
@@ -67,15 +67,16 @@ def tile_attend_x_draft_cap_topk_kernel(tc, qT, kT, vT, vs, pos, qpos, offs, out
 
         pos_g = keep.tile([P, N], F32, name="pos_g")
         seen = keep.tile([P, N], F32, name="seen")
-        bound = keep.tile([P, N], F32, name="bound")
+        bound = keep.tile([P, N], F32, name="bound", tag="q_raw")
         k_pairs = [keep.tile([P, 2 * T], BF16, name=f"k_pairs{u}", align_bytes=64) for u in range(2)]
-        k_got = keep.tile([P, PACK * N], BF16, name="k_got", align_bytes=64)
+        k_got = keep.tile([P, PACK * N], BF16, name="k_got", tag="k_got", align_bytes=64)
         k_got_words = k_got[:].bitcast(U32).rearrange("p (s u) -> p s u", u=2)
         v_pairs = keep.tile([P, 2 * T], BF16, name="v_pairs", align_bytes=64)
         v_got = keep.tile([P, 2 * N], BF16, name="v_got", align_bytes=64)
         v_words = v_got[:].bitcast(F32)
         v_turned = psum.tile([P, PACK, P], F32, name="v_turned")
-        v_bf = keep.tile([P, DV * PACK], BF16, name="v_bf", align_bytes=64)
+        visible = keep.tile([NQ, N], F32, name="visible", tag="visible", align_bytes=64)
+        v_bf = keep.tile([P, DV * PACK], BF16, name="v_bf", tag="visible", align_bytes=64)
         v_codes = keep.tile([P, DV], U32, name="v_codes", align_bytes=64)
         v_scales = keep.tile([P, DV], U8, name="v_scales", align_bytes=64)
         q_bf = keep.tile([P, NQ * PACK], BF16, name="q_bf", align_bytes=64)
@@ -84,9 +85,8 @@ def tile_attend_x_draft_cap_topk_kernel(tc, qT, kT, vT, vs, pos, qpos, offs, out
         k_codes = [keep.tile([P, HALF], U32, name=f"k_codes{h}", align_bytes=64) for h in range(2)]
         k_scales = [keep.tile([P, HALF], U8, name=f"k_scales{h}", align_bytes=64) for h in range(2)]
         score = [psum.tile([NQ, HALF], F32, name=f"score{h}") for h in range(2)]
-        vs_g = keep.tile([P, N], F32, name="vs_g")
+        vs_g = keep.tile([P, N], F32, name="vs_g", tag="k_got", align_bytes=64)
         capped = keep.tile([NQ, N], F32, name="capped")
-        visible = keep.tile([NQ, N], F32, name="visible")
         neg_max = keep.tile([NQ, 1], F32, name="neg_max")
         prob = keep.tile([NQ, N], F32, name="prob")
         sums = [keep.tile([NQ, 1], F32, name=f"row_sum{h}") for h in range(2)]
@@ -129,15 +129,17 @@ def tile_attend_x_draft_cap_topk_kernel(tc, qT, kT, vT, vs, pos, qpos, offs, out
 
         nc.vector.tensor_copy(pos_g[:], pos_pool[:].indirect(offsets[:]))
         nc.vector.tensor_scalar(out=seen[:], in0=pos_g[:], scalar1=qpos_col[:, 0:1], scalar2=CAP - MASKED, op0=ALU.is_le, op1=ALU.mult)
-        nc.scalar.activation(out=bound[:], in_=seen[:], func=ACT.Copy, bias=MASKED)
-        cast("vector", k_pairs[0], k_raw[0, 0], 0 * CHUNK, 0, 512)
-        cast("vector", k_pairs[0], k_raw[0, 1], 1 * CHUNK, 0, 512)
+        cast("scalar", k_pairs[0], k_raw[0, 0], 0 * CHUNK, 128, 512)
+        cast("vector", k_pairs[0], k_raw[0, 0], 0 * CHUNK, 0, 128)
+        cast("vector", k_pairs[0], k_raw[0, 1], 1 * CHUNK, 0, 384)
+        cast("scalar", k_pairs[0], k_raw[0, 1], 1 * CHUNK, 384, 512)
         nc.vector.tensor_copy(k_got_words[:, :, 0], k_pairs[0][:].bitcast(U32).indirect(offsets[:]))
         cast("scalar", k_pairs[1], k_raw[1, 0], 0 * CHUNK, 0, 512)
         cast("vector", k_pairs[1], k_raw[1, 1], 1 * CHUNK, 0, 384)
         cast("scalar", k_pairs[1], k_raw[1, 1], 1 * CHUNK, 384, 512)
         gather_k1(1)
         nc.scalar.copy(out=q_bf[:].rearrange("p (q j) -> p q j", j=PACK), in_=q_raw[:].rearrange("p j q -> p q j"))
+        nc.scalar.activation(out=bound[:], in_=seen[:], func=ACT.Copy, bias=MASKED)
         quant_k(1)
         nc.vector.quantize_mx(out=q_codes[:].bitcast(FP8X4), scales=q_scales[:], in_=q_bf[:])
         gather_k1(0)
@@ -162,12 +164,17 @@ def tile_attend_x_draft_cap_topk_kernel(tc, qT, kT, vT, vs, pos, qpos, offs, out
         for u in range(2):
             nc.tensor.transpose(w_turned[:, u, :], w_words[:, u::2], ident[:])
         nc.scalar.copy(
-            out=v_bf[:].rearrange("p (e t) -> p e t", t=PACK),
-            in_=v_turned[:].rearrange("p t w -> p (t w)").bitcast(BF16).rearrange("p (t e) -> p e t", t=PACK),
+            out=v_bf[:, 0:512].rearrange("p (e t) -> p e t", t=PACK),
+            in_=v_turned[:].rearrange("p t w -> p (t w)").bitcast(BF16).rearrange("p (t e) -> p e t", t=PACK)[:, 0:128, :],
+        )
+        nc.scalar.copy(
+            out=v_bf[:, 512:1024].rearrange("p (e t) -> p e t", t=PACK),
+            in_=v_turned[:].rearrange("p t w -> p (t w)").bitcast(BF16).rearrange("p (t e) -> p e t", t=PACK)[:, 128:256, :],
         )
         nc.vector.tensor_copy(out=w_bf[:].bitcast(F32).rearrange("p (q u) -> p q u", u=2), in_=w_turned[:].rearrange("p u q -> p q u"))
         nc.vector.quantize_mx(out=w_codes[:].bitcast(FP8X4), scales=w_scales[:], in_=w_bf[:])
-        nc.vector.quantize_mx(out=v_codes[:].bitcast(FP8X4), scales=v_scales[:], in_=v_bf[:])
+        nc.vector.quantize_mx(out=v_codes[:, 0:128].bitcast(FP8X4), scales=v_scales[:, 0:128], in_=v_bf[:, 0:512])
+        nc.vector.quantize_mx(out=v_codes[:, 128:256].bitcast(FP8X4), scales=v_scales[:, 128:256], in_=v_bf[:, 512:1024])
         nc.vector.tensor_tensor(out=row_sum[:], in0=sums[0][:], in1=sums[1][:], op=ALU.add)
         nc.vector.reciprocal(out=inverse[:], in_=row_sum[:])
         nc.tensor.matmul_mx(

from contextlib import ExitStack

import concourse.mybir as mybir
from concourse.masks import make_identity

D, T, N, DV, NQ = 512, 1024, 512, 256, 128
CAP = 2.0
MASKED = -30000.0
FLOPS = 2 * D * NQ * N + 2 * N * NQ * DV

P = 128
PACK = 4
HALF = N // 2
CHUNK = T // 2

F32 = mybir.dt.float32
BF16 = mybir.dt.bfloat16
U32 = mybir.dt.uint32
U16 = mybir.dt.uint16
U8 = mybir.dt.uint8
FP8X4 = mybir.dt.float8_e4m3fn_x4
ALU = mybir.AluOpType
ACT = mybir.ActivationFunctionType
AX = mybir.AxisListType


def tile_attend_x_draft_cap_topk_kernel(tc, qT, kT, vT, vs, pos, qpos, offs, out):
    nc = tc.nc
    with ExitStack() as ctx:
        keep = ctx.enter_context(tc.tile_pool(name="keep", bufs=1))
        psum = ctx.enter_context(tc.psum_pool(name="psum", bufs=1))

        offsets = keep.tile([P, N // 16], U16, name="offsets")
        qpos_col = keep.tile([P, 1], F32, name="qpos_col")
        pos_pool = keep.tile([P, T], F32, name="pos_pool")
        vs_pool = keep.tile([P, T], F32, name="vs_pool")
        q_raw = keep.tile([P, PACK, NQ], F32, name="q_raw", tag="q_raw")
        k_rows = kT.rearrange("(p j) t -> p j t", j=PACK)
        v_rows = vT.rearrange("(p h) t -> p h t", h=2)
        k_raw = {(u, c): keep.tile([P, 2, CHUNK], F32, name=f"k_raw{u}{c}") for u in range(2) for c in range(2)}
        v_raw = [keep.tile([P, 2, CHUNK], F32, name=f"v_raw{c}") for c in range(2)]

        def load_k(u, c):
            nc.sync.dma_start(out=k_raw[u, c][:], in_=k_rows[:, 2 * u : 2 * u + 2, c * CHUNK : (c + 1) * CHUNK])

        def load_v(c):
            nc.sync.dma_start(out=v_raw[c][:], in_=v_rows[:, :, c * CHUNK : (c + 1) * CHUNK])

        nc.sync.dma_start(out=pos_pool[:], in_=pos)
        nc.sync.dma_start(offsets[:], offs)
        load_k(0, 0)
        load_k(0, 1)
        load_k(1, 0)
        load_k(1, 1)
        nc.sync.dma_start(out=qpos_col[:], in_=qpos.rearrange("b q o -> (b q) o"))
        nc.sync.dma_start(out=q_raw[:], in_=qT.rearrange("b (p j) q -> p (b j) q", j=PACK))
        load_v(0)
        nc.sync.dma_start(out=vs_pool[:], in_=vs)
        load_v(1)

        warm = keep.tile([P, 1], F32, name="warm")
        nc.gpsimd.memset(warm[:], 0.0)
        warm_out = keep.tile([P, 1], F32, name="warm_out")
        nc.scalar.activation(out=warm_out[:], in_=warm[:], func=ACT.Exp)
        ident = keep.tile([P, P], F32, name="ident")
        make_identity(nc, ident[:])

        pos_g = keep.tile([P, N], F32, name="pos_g")
        seen = keep.tile([P, N], F32, name="seen")
        bound = keep.tile([P, N], F32, name="bound", tag="q_raw")
        k_pairs = [keep.tile([P, 2 * T], BF16, name=f"k_pairs{u}", align_bytes=64) for u in range(2)]
        k_got = keep.tile([P, PACK * N], BF16, name="k_got", tag="k_got", align_bytes=64)
        k_got_words = k_got[:].bitcast(U32).rearrange("p (s u) -> p s u", u=2)
        v_pairs = keep.tile([P, 2 * T], BF16, name="v_pairs", align_bytes=64)
        v_got = keep.tile([P, 2 * N], BF16, name="v_got", align_bytes=64)
        v_words = v_got[:].bitcast(F32)
        v_turned = psum.tile([P, PACK, P], F32, name="v_turned")
        visible = keep.tile([NQ, N], F32, name="visible", tag="visible", align_bytes=64)
        v_bf = keep.tile([P, DV * PACK], BF16, name="v_bf", tag="visible", align_bytes=64)
        v_codes = keep.tile([P, DV], U32, name="v_codes", align_bytes=64)
        v_scales = keep.tile([P, DV], U8, name="v_scales", align_bytes=64)
        q_bf = keep.tile([P, NQ * PACK], BF16, name="q_bf", align_bytes=64)
        q_codes = keep.tile([P, NQ], U32, name="q_codes", align_bytes=64)
        q_scales = keep.tile([P, NQ], U8, name="q_scales", align_bytes=64)
        k_codes = [keep.tile([P, HALF], U32, name=f"k_codes{h}", align_bytes=64) for h in range(2)]
        k_scales = [keep.tile([P, HALF], U8, name=f"k_scales{h}", align_bytes=64) for h in range(2)]
        score = [psum.tile([NQ, HALF], F32, name=f"score{h}") for h in range(2)]
        vs_g = keep.tile([P, N], F32, name="vs_g", tag="k_got", align_bytes=64)
        capped = keep.tile([NQ, N], F32, name="capped")
        neg_max = keep.tile([NQ, 1], F32, name="neg_max")
        prob = keep.tile([NQ, N], F32, name="prob")
        sums = [keep.tile([NQ, 1], F32, name=f"row_sum{h}") for h in range(2)]
        weight = keep.tile([NQ, N], BF16, name="weight", align_bytes=64)
        w_turned = psum.tile([P, 2, NQ], F32, name="w_turned")
        w_words = weight[:].bitcast(F32)
        w_bf = keep.tile([P, NQ * PACK], BF16, name="w_bf", align_bytes=64)
        w_codes = keep.tile([P, NQ], U32, name="w_codes", align_bytes=64)
        w_scales = keep.tile([P, NQ], U8, name="w_scales", align_bytes=64)
        row_sum = keep.tile([NQ, 1], F32, name="row_sum")
        inverse = keep.tile([NQ, 1], F32, name="inverse")
        y = psum.tile([NQ, DV], F32, name="y")
        result = keep.tile([NQ, DV], F32, name="result")

        def cast(engine, pairs, raw, first, a, b):
            dst = pairs[:, 2 * (first + a) : 2 * (first + b)].rearrange("p (t h) -> p t h", h=2)
            src = raw[:, :, a:b].rearrange("p h t -> p t h")
            if engine == "scalar":
                nc.scalar.copy(out=dst, in_=src)
            else:
                nc.vector.tensor_copy(out=dst, in_=src)

        def half(h):
            return slice(h * HALF, (h + 1) * HALF)

        def mul_scores(h):
            nc.tensor.matmul_mx(
                out=score[h][:], lhsT=q_codes[:].bitcast(FP8X4), lhsT_scale=q_scales[:],
                rhs=k_codes[h][:].bitcast(FP8X4), rhs_scale=k_scales[h][:], start=True, stop=True,
            )

        def gather_k1(h):
            nc.vector.tensor_copy(
                k_got_words[:, half(h), 1],
                k_pairs[1][:].bitcast(U32).indirect(offsets[:, h * HALF // 16 : (h + 1) * HALF // 16]),
            )

        def quant_k(h):
            nc.vector.quantize_mx(out=k_codes[h][:].bitcast(FP8X4), scales=k_scales[h][:], in_=k_got[:, h * PACK * HALF : (h + 1) * PACK * HALF])

        nc.vector.tensor_copy(pos_g[:], pos_pool[:].indirect(offsets[:]))
        nc.vector.tensor_scalar(out=seen[:], in0=pos_g[:], scalar1=qpos_col[:, 0:1], scalar2=CAP - MASKED, op0=ALU.is_le, op1=ALU.mult)
        cast("scalar", k_pairs[0], k_raw[0, 0], 0 * CHUNK, 128, 512)
        cast("vector", k_pairs[0], k_raw[0, 0], 0 * CHUNK, 0, 128)
        cast("vector", k_pairs[0], k_raw[0, 1], 1 * CHUNK, 0, 384)
        cast("scalar", k_pairs[0], k_raw[0, 1], 1 * CHUNK, 384, 512)
        nc.vector.tensor_copy(k_got_words[:, :, 0], k_pairs[0][:].bitcast(U32).indirect(offsets[:]))
        cast("scalar", k_pairs[1], k_raw[1, 0], 0 * CHUNK, 0, 512)
        cast("vector", k_pairs[1], k_raw[1, 1], 1 * CHUNK, 0, 384)
        cast("scalar", k_pairs[1], k_raw[1, 1], 1 * CHUNK, 384, 512)
        gather_k1(1)
        nc.scalar.copy(out=q_bf[:].rearrange("p (q j) -> p q j", j=PACK), in_=q_raw[:].rearrange("p j q -> p q j"))
        nc.scalar.activation(out=bound[:], in_=seen[:], func=ACT.Copy, bias=MASKED)
        quant_k(1)
        nc.vector.quantize_mx(out=q_codes[:].bitcast(FP8X4), scales=q_scales[:], in_=q_bf[:])
        gather_k1(0)
        quant_k(0)
        mul_scores(0)
        mul_scores(1)
        cast("scalar", v_pairs, v_raw[0], 0 * CHUNK, 0, 512)
        nc.vector.tensor_copy(vs_g[:], vs_pool[:].indirect(offsets[:]))
        nc.scalar.activation(out=capped[:, half(0)], in_=score[0][:], func=ACT.Tanh, scale=1.0 / CAP)
        nc.scalar.activation(out=capped[:, half(1)], in_=score[1][:], func=ACT.Tanh, scale=1.0 / CAP)
        nc.vector.scalar_tensor_tensor(out=visible[:, half(0)], in0=capped[:, half(0)], scalar=CAP, in1=bound[:, half(0)], op0=ALU.mult, op1=ALU.min)
        nc.vector.scalar_tensor_tensor(out=visible[:, half(1)], in0=capped[:, half(1)], scalar=CAP, in1=bound[:, half(1)], op0=ALU.mult, op1=ALU.min)
        nc.vector.tensor_reduce(out=neg_max[:], in_=visible[:], axis=AX.X, op=ALU.max, negate=True)
        cast("scalar", v_pairs, v_raw[1], 1 * CHUNK, 0, 512)
        nc.scalar.activation(out=prob[:, half(0)], in_=visible[:, half(0)], func=ACT.Exp, bias=neg_max[:, 0:1], accum_out=sums[0][:])
        nc.scalar.activation(out=prob[:, half(1)], in_=visible[:, half(1)], func=ACT.Exp, bias=neg_max[:, 0:1], accum_out=sums[1][:])
        nc.vector.tensor_copy(v_got[:].bitcast(U32).rearrange("p (t s) -> p s t", t=PACK), v_pairs[:].bitcast(U32).indirect(offsets[:]))
        for t in range(PACK):
            nc.tensor.transpose(v_turned[:, t, :], v_words[:, t * P : (t + 1) * P], ident[:])
        nc.vector.tensor_tensor(out=weight[:, half(0)], in0=prob[:, half(0)], in1=vs_g[:, half(0)], op=ALU.mult)
        nc.vector.tensor_tensor(out=weight[:, half(1)], in0=prob[:, half(1)], in1=vs_g[:, half(1)], op=ALU.mult)
        for u in range(2):
            nc.tensor.transpose(w_turned[:, u, :], w_words[:, u::2], ident[:])
        nc.scalar.copy(
            out=v_bf[:, 0:512].rearrange("p (e t) -> p e t", t=PACK),
            in_=v_turned[:].rearrange("p t w -> p (t w)").bitcast(BF16).rearrange("p (t e) -> p e t", t=PACK)[:, 0:128, :],
        )
        nc.scalar.copy(
            out=v_bf[:, 512:1024].rearrange("p (e t) -> p e t", t=PACK),
            in_=v_turned[:].rearrange("p t w -> p (t w)").bitcast(BF16).rearrange("p (t e) -> p e t", t=PACK)[:, 128:256, :],
        )
        nc.vector.tensor_copy(out=w_bf[:].bitcast(F32).rearrange("p (q u) -> p q u", u=2), in_=w_turned[:].rearrange("p u q -> p q u"))
        nc.vector.quantize_mx(out=w_codes[:].bitcast(FP8X4), scales=w_scales[:], in_=w_bf[:])
        nc.vector.quantize_mx(out=v_codes[:, 0:128].bitcast(FP8X4), scales=v_scales[:, 0:128], in_=v_bf[:, 0:512])
        nc.vector.quantize_mx(out=v_codes[:, 128:256].bitcast(FP8X4), scales=v_scales[:, 128:256], in_=v_bf[:, 512:1024])
        nc.vector.tensor_tensor(out=row_sum[:], in0=sums[0][:], in1=sums[1][:], op=ALU.add)
        nc.vector.reciprocal(out=inverse[:], in_=row_sum[:])
        nc.tensor.matmul_mx(
            out=y[:], lhsT=w_codes[:].bitcast(FP8X4), lhsT_scale=w_scales[:],
            rhs=v_codes[:].bitcast(FP8X4), rhs_scale=v_scales[:], start=True, stop=True,
        )
        nc.vector.tensor_scalar(out=result[:], in0=y[:], scalar1=inverse[:, 0:1], scalar2=None, op0=ALU.mult)
        nc.sync.dma_start(out=out.rearrange("b q e -> (b q) e"), in_=result[:])
